import numpy as np
import ml_dtypes


def mxq(x, axis, fmt="e4m3"):
    dtype, down = {"e4m3": (ml_dtypes.float8_e4m3fn, 7), "e5m2": (ml_dtypes.float8_e5m2, 14)}[fmt]
    v = np.moveaxis(np.asarray(x, np.float32).astype(ml_dtypes.bfloat16).astype(np.float64), axis, -1)
    blocks = v.reshape(v.shape[:-1] + (-1, 32))
    amax = np.abs(blocks).max(-1, keepdims=True)
    byte = np.maximum(np.where(amax > 0, np.frexp(amax)[1] - 1 + 127, 0) - down, 1)
    scale = np.exp2(byte - 127.0)
    codes = (blocks / scale).astype(np.float32).astype(dtype).astype(np.float64)
    return np.moveaxis((codes * scale).reshape(v.shape), -1, axis)


WIDE = False


def mx_kscale(k):
    if not WIDE:
        return np.ones(k)
    levels = np.array([10, -10, 5, -5, 0])
    if k % 512:
        return np.exp2(np.random.permutation(np.resize(levels, k // 32))).repeat(32)
    a = np.empty((k // 512, 16))
    for p in range(k // 512):
        a[p, :8] = np.random.permutation(np.resize(levels, 8))
        for g in range(8):
            far = levels[np.abs(levels - a[p, g]) >= 10]
            a[p, g + 8] = far[np.random.randint(len(far))]
    return np.exp2(a.ravel()).repeat(32)


BF16 = ml_dtypes.bfloat16


def bf(x):
    return np.asarray(x, np.float32).astype(BF16)


def f64(x):
    return np.asarray(x).astype(np.float64)


N, I, D, R = 2048, 512, 512, 1024


def sigmoid(v):
    return 1.0 / (1.0 + np.exp(-v))


def draw0():
    s, v, t = mx_kscale(I), mx_kscale(D), mx_kscale(N)
    return {"x": bf(np.random.standard_normal((N, I)) * s),
            "h": bf(np.tanh(np.random.standard_normal((N, D))) * v),
            "w": bf(np.random.standard_normal((I, 3 * D)) / np.sqrt(I) / s[:, None]),
            "u": bf(np.random.standard_normal((D, 3 * D)) / np.sqrt(D) / v[:, None]),
            "b": bf(0.5 * np.random.standard_normal(3 * D)),
            "c": bf(0.5 * np.random.standard_normal(D)),
            "carry": bf((1.0 + 0.1 * np.random.standard_normal(D)) / v),
            "gain": bf((1.0 + 0.1 * np.random.standard_normal(N)) * t),
            "p": bf(np.random.standard_normal((R, N)) / np.sqrt(N) / t),
            "o": bf(0.3 * np.random.standard_normal(R))}


def core(x, h, w, u, b, c, carry, gain, p, o):
    hs = f64(h)
    a = (mxq(f64(x), 1, "e4m3") @ mxq(f64(w), 0, "e4m3")) + f64(b)
    e = mxq(hs, 1, "e4m3") @ mxq(f64(u), 0, "e4m3")
    r = sigmoid(a[:, :D] + e[:, :D])
    z = sigmoid(a[:, D:2 * D] + e[:, D:2 * D])
    n = np.tanh(a[:, 2 * D:] + r * (e[:, 2 * D:] + f64(c)))
    h_new = (1.0 - z) * n + z * (hs * f64(carry))
    m = h_new * f64(gain)[:, None]
    y = (mxq(f64(p), 1, "e4m3") @ mxq(m, 0, "e4m3")) + f64(o)[:, None]
    return y, h_new


def e4m3fn_bytes(y):
    return np.clip(np.asarray(y, np.float64), -448.0, 448.0).astype(np.float32).astype(ml_dtypes.float8_e4m3fn).view(np.uint8)


def e4m3fn_values(b):
    return np.asarray(b, np.uint8).view(ml_dtypes.float8_e4m3fn).astype(np.float64)


def setup_inputs():
    d = draw0()
    x0 = np.asarray(d['p']).astype(np.float64)
    s = (np.max(np.abs(x0), axis=(0,), keepdims=True) / 448.0).astype(np.float32)
    out = {}
    for k, v in d.items():
        if k == 'p':
            out['p_bytes'] = e4m3fn_bytes(x0 / s.astype(np.float64))
            out['p_scale'] = s
        else:
            out[k] = v
    return out


def reference(x, h, w, u, b, c, carry, gain, p_bytes, p_scale, o):
    return core(x, h, w, u, b, c, carry, gain, e4m3fn_values(p_bytes) * p_scale.astype(np.float64), o)

@@ -1,0 +1,417 @@
+from contextlib import ExitStack
+
+import concourse.mybir as mybir
+from concourse.masks import make_identity
+
+N, I, D, R = 2048, 512, 512, 1024
+FLOPS = 2 * N * (I + D) * 3 * D + 2 * R * N * D
+
+F32 = mybir.dt.float32
+BF16 = mybir.dt.bfloat16
+U32 = mybir.dt.uint32
+U8 = mybir.dt.uint8
+FP8 = mybir.dt.float8_e4m3fn
+FP8X4 = mybir.dt.float8_e4m3fn_x4
+ACT = mybir.ActivationFunctionType
+ALU = mybir.AluOpType
+
+P = 128
+G = 4
+C = 4
+S = 8
+TILES = G * C
+RESET, UPDATE, CAND = 0, 1, 2
+M_ENGINE = "vvvvvvvvvvvvvvvv"
+
+
+def tile_gru_station_readout_f4_kernel(
+    tc, x, h, w, u, b, c, carry, gain, p_bytes, p_scale, o, y, h_new
+):
+    nc = tc.nc
+    with ExitStack() as ctx:
+        const = ctx.enter_context(tc.tile_pool(name="const", bufs=1))
+        pool = ctx.enter_context(tc.tile_pool(name="pool", bufs=2))
+        psum = ctx.enter_context(tc.psum_pool(name="psum", bufs=1))
+
+        ident = const.tile([P, P], F32, name="ident")
+        ident_b = const.tile([P, P], BF16, name="ident_b")
+        vec_rows = const.tile([P, P], BF16, name="vec_rows")
+        vec = const.tile([P, P], F32, name="vec")
+        gain_b = const.tile([P, G, 4], BF16, name="gain_b")
+        gain_f = const.tile([P, G, 4], F32, name="gain_f")
+        o_col = const.tile([P, S], BF16, name="o_col")
+        scale_rows = const.tile([P, N], F32, name="scale_rows")
+        warm = const.tile([P, 1], F32, name="warm")
+
+        def bank(tag, bufs=1, dtype=F32):
+            return psum.tile([P, 512], dtype, name="bank_" + tag, tag=tag, bufs=bufs)
+
+        def copy(engine, out, in_):
+            if engine == "s":
+                nc.scalar.copy(out, in_)
+            else:
+                nc.vector.tensor_copy(out=out, in_=in_)
+
+        def mx(out, lhs, lhs_cols, rhs, start, stop):
+            nc.tensor.matmul_mx(
+                out=out,
+                lhsT=lhs[0][:, lhs_cols].bitcast(FP8X4),
+                lhsT_scale=lhs[1][:, lhs_cols],
+                rhs=rhs[0][:].bitcast(FP8X4),
+                rhs_scale=rhs[1][:],
+                start=start,
+                stop=stop,
+            )
+
+        def operand(home, tag, bufs):
+            codes = home.tile([P, 512], U32, name=tag + "_codes", bufs=bufs, align_bytes=64)
+            scales = home.tile([P, 512], U8, name=tag + "_scales", bufs=bufs, align_bytes=64)
+            return codes, scales
+
+        def quantize(target, cols, in_):
+            nc.vector.quantize_mx(
+                out=target[0][:, cols].bitcast(FP8X4), scales=target[1][:, cols], in_=in_
+            )
+
+        raws = {}
+
+        def load_rows(name, src, g, bufs):
+            raw = pool.tile([P, 4, 512], BF16, name=name + "_raw", bufs=bufs)
+            nc.sync.dma_start(out=raw[:], in_=src.rearrange("(g p t) k -> g p t k", p=P, t=4)[g])
+            raws[name, g] = raw
+
+        def load_weight(name, src, th):
+            raw = const.tile([P, 4, 512], BF16, name=name + "_raw" + str(th))
+            nc.sync.dma_start(
+                out=raw[:],
+                in_=src.rearrange("(p j) n -> p j n", j=4)[:, :, 512 * th : 512 * th + 512],
+            )
+            raws[name, th] = raw
+
+        def load_p(pair):
+            raw = pool.tile([P, 2, N], U8, name="p_raw", bufs=4)
+            nc.sync.dma_start(
+                out=raw[:], in_=p_bytes.rearrange("(p s) k -> p s k", s=S)[:, 2 * pair : 2 * pair + 2, :]
+            )
+            raws["p", pair] = raw
+
+        nc.vector.memset(warm[:], 0.0)
+        nc.vector.memset(vec_rows[:], 0.0)
+        nc.scalar.activation(warm[:], warm[:], ACT.Sigmoid)
+        make_identity(nc, ident[:])
+        nc.vector.tensor_copy(out=ident_b[:], in_=ident[:])
+        load_rows("x", x, 0, 2)
+        load_rows("h", h, 0, 3)
+        nc.scalar.dma_start(out=vec_rows[0:12, :], in_=b.rearrange("(r m) -> r m", m=P))
+        nc.scalar.dma_start(out=vec_rows[12:16, :], in_=c.rearrange("(r m) -> r m", m=P))
+        nc.scalar.dma_start(out=vec_rows[16:20, :], in_=carry.rearrange("(r m) -> r m", m=P))
+        nc.gpsimd.dma_start(out=gain_b[:], in_=gain.rearrange("(g p t) -> p g t", p=P, t=4))
+        nc.gpsimd.dma_start(out=o_col[:], in_=o.rearrange("(p s) -> p s", s=S))
+        for th in (RESET, CAND, UPDATE):
+            load_weight("w", w, th)
+            load_weight("u", u, th)
+        load_rows("x", x, 1, 2)
+        load_rows("h", h, 1, 3)
+        nc.sync.dma_start(
+            out=scale_rows[:], in_=p_scale.rearrange("o k -> (o k)").partition_broadcast(P)
+        )
+        load_p(0)
+        load_p(1)
+        load_rows("x", x, 2, 2)
+        load_rows("h", h, 2, 3)
+        load_p(2)
+        load_p(3)
+        load_rows("x", x, 3, 2)
+        load_rows("h", h, 3, 3)
+
+        ops = {}
+        grouped = {}
+
+        def unit_transposes(key, rows, half):
+            if half == 0:
+                grouped[key] = pool.tile([P, 2048], BF16, name=key[0] + "_grouped", bufs=2, align_bytes=64)
+            words = rows.bitcast(F32)
+            tp = bank("tp", 2)
+            for k in range(4):
+                base = 256 * (2 * half + k // 2) + k % 2
+                end = 256 * (2 * half + k // 2) + 256
+                nc.tensor.transpose(tp[:, 128 * k : 128 * k + 128], words[:, base:end:2], ident[:])
+            return key, half, tp
+
+        def unit_copy(engine, unit):
+            key, half, tp = unit
+            copy(
+                engine,
+                grouped[key][:].bitcast(F32)[:, 512 * half : 512 * half + 512].rearrange(
+                    "p (a r e) -> p a r e", a=2, e=2
+                ),
+                tp[:].rearrange("p (a e r) -> p a r e", a=2, e=2),
+            )
+
+        def unit_rows(key):
+            if key[0] == "p":
+                return raws["p_rows", key[1]][:]
+            return raws[key][:].rearrange("p t k -> p (t k)")
+
+        def quantize_grouped(key):
+            ops[key] = operand(const if key[0] == "p" else pool, key[0] + (str(key[1]) if key[0] == "p" else ""), 1 if key[0] == "p" else 2)
+            quantize(ops[key], slice(0, 512), grouped[key][:])
+
+        def product(s, half):
+            if half == 0:
+                raws["p_rows", s] = pool.tile([P, N], BF16, name="p_rows", bufs=2, align_bytes=64)
+            cols = slice(1024 * half, 1024 * half + 1024)
+            nc.vector.tensor_tensor(
+                out=raws["p_rows", s][:, cols],
+                in0=raws["p", s // 2][:, s % 2, cols].bitcast(FP8),
+                in1=scale_rows[:, cols],
+                op=ALU.mult,
+            )
+
+        def weight_copy(name, th, pair, engine):
+            if pair == 0:
+                ops[name, th] = operand(const, name + str(th), 1)
+            wg = pool.tile([P, 1024], BF16, name="weight_grouped", bufs=3, align_bytes=64)
+            copy(
+                engine,
+                wg[:].rearrange("p (m j) -> p m j", j=4),
+                raws[name, th][:, :, 256 * pair : 256 * pair + 256].rearrange("p j m -> p m j"),
+            )
+            return name, th, pair, wg
+
+        def weight_quantize(piece):
+            name, th, pair, wg = piece
+            quantize(ops[name, th], slice(256 * pair, 256 * pair + 256), wg[:])
+
+        acc = {}
+        live = {}
+
+        def gates_matmul(i):
+            g, cc = divmod(i, C)
+            cols = slice(128 * cc, 128 * cc + 128)
+            xq, hq = ops["x", g], ops["h", g]
+            acc[0] = bank("acc0")
+            mx(acc[0][:], ops["w", RESET], cols, xq, True, False)
+            mx(acc[0][:], ops["u", RESET], cols, hq, False, True)
+            acc[1] = bank("acc1")
+            mx(acc[1][:], ops["u", CAND], cols, hq, True, True)
+            acc[2] = bank("acc2")
+            mx(acc[2][:], ops["w", CAND], cols, xq, True, True)
+            acc[3] = bank("acc3")
+            mx(acc[3][:], ops["w", UPDATE], cols, xq, True, False)
+            mx(acc[3][:], ops["u", UPDATE], cols, hq, False, True)
+
+        def ew(name, bufs):
+            return pool.tile([P, 512], F32, name=name, bufs=bufs)
+
+        def vcol(r):
+            return vec[:, r : r + 1]
+
+        def gate_r(i):
+            r = ew("r_gate", 2)
+            nc.scalar.activation(r[:], acc[0][:], ACT.Sigmoid, bias=vcol(i % C))
+            live["r", i] = r
+
+        def gate_z(i):
+            z = ew("z_gate", 3)
+            nc.scalar.activation(z[:], acc[3][:], ACT.Sigmoid, bias=vcol(4 + i % C))
+            live["z", i] = z
+
+        def step_s1(i):
+            s1 = ew("s1", 2)
+            nc.vector.scalar_tensor_tensor(
+                out=s1[:], in0=acc[1][:], scalar=vcol(12 + i % C), in1=live["r", i][:], op0=ALU.add, op1=ALU.mult
+            )
+            live["s1", i] = s1
+
+        def step_s2(i):
+            s2 = ew("s2", 2)
+            nc.vector.tensor_tensor(out=s2[:], in0=acc[2][:], in1=live["s1", i][:], op=ALU.add)
+            live["s2", i] = s2
+
+        def step_n(i):
+            n = ew("n_cand", 4)
+            nc.scalar.activation(n[:], live["s2", i][:], ACT.Tanh, bias=vcol(8 + i % C))
+            live["n", i] = n
+
+        def h_transposes(i):
+            g, cc = divmod(i, C)
+            ht = bank("ht", 1, BF16)
+            for t in range(4):
+                nc.tensor.transpose(
+                    ht[:, 128 * t : 128 * t + 128],
+                    raws["h", g][:, t, 128 * cc : 128 * cc + 128],
+                    ident_b[:],
+                )
+            live["ht", i] = ht
+
+        def step_d(i):
+            d = ew("diff", 2)
+            nc.vector.scalar_tensor_tensor(
+                out=d[:], in0=live["ht", i][:], scalar=vcol(16 + i % C), in1=live["n", i][:],
+                op0=ALU.mult, op1=ALU.subtract,
+            )
+            live["d", i] = d
+
+        def step_q(i, engine):
+            q = ew("zdiff", 3)
+            engine.tensor_tensor(out=q[:], in0=live["z", i][:], in1=live["d", i][:], op=ALU.mult)
+            live["q", i] = q
+
+        def state_transposes(i):
+            hb = bank("hb")
+            for t in range(4):
+                cols = slice(128 * t, 128 * t + 128)
+                for k, part in enumerate(("n", "q")):
+                    nc.tensor.matmul(
+                        hb[:, cols], lhsT=live[part, i][:, cols], rhs=ident[:],
+                        start=(k == 0), stop=(k == 1), is_transpose=True,
+                    )
+            live["hb", i] = hb
+
+        h_out = h_new.rearrange("(g p t) d -> g p t d", p=P, t=4)
+        hn = {}
+
+        def state_copy(i):
+            g, cc = divmod(i, C)
+            if cc == 0:
+                hn[g] = pool.tile([P, 4, 512], F32, name="hn", bufs=2)
+            nc.scalar.copy(
+                hn[g][:, :, 128 * cc : 128 * cc + 128], live["hb", i][:].rearrange("p (t j) -> p t j", t=4)
+            )
+
+        def state_store(g):
+            nc.sync.dma_start(out=h_out[g], in_=hn[g][:])
+
+        def step_m(i, engine):
+            g, cc = divmod(i, C)
+            mg = pool.tile([P, 512], BF16, name="m_grouped", bufs=3, align_bytes=64)
+            if engine == "v":
+                source = live["hb", i][:].rearrange("p (t j) -> p j t", t=4)
+                nc.vector.tensor_tensor(
+                    out=mg[:].rearrange("p (j t) -> p j t", t=4), in0=source,
+                    in1=gain_f[:, g, :].unsqueeze(1).to_broadcast([P, P, 4]), op=ALU.mult,
+                )
+            else:
+                source = hn[g][:, :, 128 * cc : 128 * cc + 128].rearrange("p t j -> p j t")
+                nc.gpsimd.tensor_tensor(
+                    out=mg[:].rearrange("p (j t) -> p j t", t=4), in0=source,
+                    in1=gain_f[:, g, :].unsqueeze(1).to_broadcast([P, P, 4]), op=ALU.mult,
+                )
+            live["m", i] = mg
+
+        def quantize_m(i):
+            g, cc = divmod(i, C)
+            if cc == 0:
+                ops["m", g] = operand(const, "m" + str(g), 1)
+            quantize(ops["m", g], slice(128 * cc, 128 * cc + 128), live["m", i][:])
+
+        y_out = y.rearrange("(p s) d -> p s d", s=S)
+        y_banks = ("acc0", "acc1", "acc2", "acc3", "tp", "tp", "ht", "hb")
+        y_acc = {}
+
+        def y_passes(s, groups):
+            if s not in y_acc:
+                y_acc[s] = bank(y_banks[s], 2 if y_banks[s] == "tp" else 1)
+            for g in groups:
+                mx(y_acc[s][:], ops["p", s], slice(128 * g, 128 * g + 128), ops["m", g], g == 0, g == G - 1)
+
+        def y_store(s):
+            ys = pool.tile([P, 512], F32, name="y_rows", bufs=8)
+            if s % 2:
+                nc.vector.tensor_scalar(
+                    out=ys[:], in0=y_acc[s][:], scalar1=o_col[:, s : s + 1], scalar2=None, op0=ALU.add
+                )
+            else:
+                nc.scalar.activation(ys[:], y_acc[s][:], ACT.Identity, bias=o_col[:, s : s + 1])
+            nc.sync.dma_start(out=y_out[:, s, :], in_=ys[:])
+
+        units = {1: (("x", 1),), 2: (("h", 1),), 4: (("p", 0),), 5: (("x", 2),), 6: (("h", 2),), 7: (("p", 1),),
+                 8: (("p", 2),), 9: (("x", 3),), 10: (("h", 3),), 11: (("p", 3),), 12: (("p", 4),), 13: (("p", 5),),
+                 14: (("p", 6), ("p", 7))}
+        counts = [0, 0, 1, 1, 1, 1, 1, 1, 1, 1, 1, 1, 3, 3, 0, 0]
+        products = [(k // 2, k % 2) for k in range(16)]
+        late_weights = {0: (RESET, CAND), 1: (UPDATE,)}
+
+        with tc.manual_schedule(
+            engines={mybir.EngineType.PE, mybir.EngineType.Activation, mybir.EngineType.DVE, mybir.EngineType.Pool}
+        ):
+            for key in (("x", 0), ("h", 0)):
+                for half in range(2):
+                    unit = unit_transposes(key, unit_rows(key), half)
+                    unit_copy("vs"[half], unit)
+            quantize_grouped(("x", 0))
+            quantize_grouped(("h", 0))
+            nc.gpsimd.tensor_copy(out=gain_f[:], in_=gain_b[:])
+            for th in (RESET, CAND, UPDATE):
+                wp = weight_copy("w", th, 0, "v")
+                up = weight_copy("u", th, 0, "s")
+                weight_quantize(wp)
+                weight_quantize(up)
+                if th == RESET:
+                    vec_ps = bank("ht", 1, BF16)
+                    nc.tensor.transpose(vec_ps[:, 0:128], vec_rows[:], ident_b[:])
+                    nc.scalar.copy(vec[:], vec_ps[:, 0:128])
+            gates_matmul(0)
+            h_transposes(0)
+
+            last = TILES - 1
+            pending = []
+            for i in range(TILES):
+                keys = units.get(i, ())
+                gate_r(i)
+                step_s1(i)
+                gate_z(i)
+                if i > 1:
+                    step_m(i - 2, M_ENGINE[i - 2])
+                step_s2(i)
+                for key in keys:
+                    for half in range(2):
+                        unit = unit_transposes(key, unit_rows(key), half)
+                        unit_copy("s", unit)
+                if i > 0:
+                    h_transposes(i)
+                    state_transposes(i - 1)
+                step_n(i)
+                if i > 0:
+                    state_copy(i - 1)
+                if i > 1:
+                    quantize_m(i - 2)
+                    if i % C == 1 and i > C:
+                        state_store(i // C - 1)
+                for old in pending:
+                    quantize_grouped(old)
+                pending = []
+                for th in late_weights.get(i, ()):
+                    wp = weight_copy("w", th, 1, "v")
+                    up = weight_copy("u", th, 1, "s")
+                    weight_quantize(wp)
+                    weight_quantize(up)
+                for k in range(counts[i]):
+                    s, half = products.pop(0)
+                    product(s, half)
+                step_d(i)
+                step_q(i, nc.gpsimd if i < last else nc.vector)
+                pending.extend(keys)
+                if i + 1 < TILES:
+                    gates_matmul(i + 1)
+                else:
+                    for s in (4, 5, 0, 1):
+                        y_passes(s, range(G - 1))
+
+            step_m(last - 1, "v")
+            quantize_m(last - 1)
+            for old in pending:
+                quantize_grouped(old)
+            state_transposes(last)
+            step_m(last, "v")
+            quantize_m(last)
+            state_copy(last)
+            state_store(G - 1)
+            for s in (2, 3, 6):
+                y_passes(s, range(G - 1))
+            for s in range(7):
+                y_passes(s, (G - 1,))
+                y_store(s)
+            y_passes(7, range(G))
+            y_store(7)

@@ -21,7 +21,16 @@ C = 4
 S = 8
 TILES = G * C
 RESET, UPDATE, CAND = 0, 1, 2
-M_ENGINE = "vvvvvvvvvvvvvvvv"
+WBUFS = 4
+XBUFS = 4
+ORDER = [(cc, g) for g in range(G) for cc in range(2)] + [(cc, g) for cc in range(2, C) for g in range(G)]
+EARLY = (('h', 1),)
+UNITS = {1: (('h', 1), ('h', 2)), 2: (('x', 2), ('x', 3)), 9: (('p', 4),), 3: (('h', 3),), 12: (('p', 6),), 8: (('p', 3),), 4: (('p', 0),), 5: (('p', 1),), 13: (('p', 7),), 10: (('p', 5),), 7: (('p', 2),), 0: (('x', 1),)}
+COUNTS = [0, 2, 1, 1, 1, 2, 1, 2, 1, 1, 1, 1, 2, 0, 0, 0]
+WEIGHT_SLOTS = {0: ((1, 0), (1, 2), (1, 1)), 6: ((3, 2), (2, 1)), 8: ((3, 0),), 7: ((3, 1),), 3: ((2, 2),), 5: ((2, 0),)}
+Y_SLOTS = {13: ((0, 2),), 14: ((1, 0),), 16: ((0, 1), (1, 2), (1, 1)), 10: ((0, 0),)}
+SLOT = 'r s1 m z u1 s2 quant w ys u0 ht n prod d mq nq mx yp hc'.split()
+W_ENGINE = "vvss"
 
 
 def tile_gru_station_readout_f4_kernel(
@@ -80,13 +89,13 @@ def tile_gru_station_readout_f4_kernel(
             nc.sync.dma_start(out=raw[:], in_=src.rearrange("(g p t) k -> g p t k", p=P, t=4)[g])
             raws[name, g] = raw
 
-        def load_weight(name, src, th):
-            raw = const.tile([P, 4, 512], BF16, name=name + "_raw" + str(th))
+        def load_weight(name, src, cc):
+            raw = pool.tile([P, 12, 128], BF16, name=name + "_raw", bufs=WBUFS)
             nc.sync.dma_start(
                 out=raw[:],
-                in_=src.rearrange("(p j) n -> p j n", j=4)[:, :, 512 * th : 512 * th + 512],
+                in_=src.rearrange("(p j) (th n) -> p (j th) n", j=4, th=3)[:, :, 128 * cc : 128 * cc + 128],
             )
-            raws[name, th] = raw
+            raws[name, "w", cc] = raw
 
         def load_p(pair):
             raw = pool.tile([P, 2, N], U8, name="p_raw", bufs=4)
@@ -100,29 +109,34 @@ def tile_gru_station_readout_f4_kernel(
         nc.scalar.activation(warm[:], warm[:], ACT.Sigmoid)
         make_identity(nc, ident[:])
         nc.vector.tensor_copy(out=ident_b[:], in_=ident[:])
-        load_rows("x", x, 0, 2)
-        load_rows("h", h, 0, 3)
+        load_rows("x", x, 0, XBUFS)
+        load_rows("h", h, 0, 4)
         nc.scalar.dma_start(out=vec_rows[0:12, :], in_=b.rearrange("(r m) -> r m", m=P))
         nc.scalar.dma_start(out=vec_rows[12:16, :], in_=c.rearrange("(r m) -> r m", m=P))
         nc.scalar.dma_start(out=vec_rows[16:20, :], in_=carry.rearrange("(r m) -> r m", m=P))
         nc.gpsimd.dma_start(out=gain_b[:], in_=gain.rearrange("(g p t) -> p g t", p=P, t=4))
         nc.gpsimd.dma_start(out=o_col[:], in_=o.rearrange("(p s) -> p s", s=S))
-        for th in (RESET, CAND, UPDATE):
-            load_weight("w", w, th)
-            load_weight("u", u, th)
-        load_rows("x", x, 1, 2)
-        load_rows("h", h, 1, 3)
+        load_weight("w", w, 0)
+        load_weight("u", u, 0)
+        load_weight("w", w, 1)
+        load_weight("u", u, 1)
+        load_rows("x", x, 1, XBUFS)
+        load_rows("h", h, 1, 4)
+        load_rows("x", x, 2, XBUFS)
+        load_rows("h", h, 2, 4)
         nc.sync.dma_start(
             out=scale_rows[:], in_=p_scale.rearrange("o k -> (o k)").partition_broadcast(P)
         )
         load_p(0)
+        load_rows("x", x, 3, XBUFS)
+        load_rows("h", h, 3, 4)
         load_p(1)
-        load_rows("x", x, 2, 2)
-        load_rows("h", h, 2, 3)
         load_p(2)
+        load_weight("w", w, 2)
+        load_weight("u", u, 2)
         load_p(3)
-        load_rows("x", x, 3, 2)
-        load_rows("h", h, 3, 3)
+        load_weight("w", w, 3)
+        load_weight("u", u, 3)
 
         ops = {}
         grouped = {}
@@ -154,7 +168,7 @@ def tile_gru_station_readout_f4_kernel(
             return raws[key][:].rearrange("p t k -> p (t k)")
 
         def quantize_grouped(key):
-            ops[key] = operand(const if key[0] == "p" else pool, key[0] + (str(key[1]) if key[0] == "p" else ""), 1 if key[0] == "p" else 2)
+            ops[key] = operand(const, key[0] + str(key[1]), 1)
             quantize(ops[key], slice(0, 512), grouped[key][:])
 
         def product(s, half):
@@ -168,38 +182,46 @@ def tile_gru_station_readout_f4_kernel(
                 op=ALU.mult,
             )
 
-        def weight_copy(name, th, pair, engine):
-            if pair == 0:
-                ops[name, th] = operand(const, name + str(th), 1)
-            wg = pool.tile([P, 1024], BF16, name="weight_grouped", bufs=3, align_bytes=64)
+        def weight_copy(name, cc, th, engine):
+            if (name, "w", cc) not in ops:
+                codes = pool.tile([P, 384], U32, name=name + "_w_codes", bufs=3, align_bytes=64)
+                scales = pool.tile([P, 384], U8, name=name + "_w_scales", bufs=3, align_bytes=64)
+                ops[name, "w", cc] = (codes, scales)
+            wg = pool.tile([P, 512], BF16, name="weight_grouped", bufs=6, align_bytes=64)
             copy(
                 engine,
                 wg[:].rearrange("p (m j) -> p m j", j=4),
-                raws[name, th][:, :, 256 * pair : 256 * pair + 256].rearrange("p j m -> p m j"),
+                raws[name, "w", cc][:].rearrange("p (j th) m -> p th m j", th=3)[:, th],
             )
-            return name, th, pair, wg
+            return name, cc, th, wg
 
         def weight_quantize(piece):
-            name, th, pair, wg = piece
-            quantize(ops[name, th], slice(256 * pair, 256 * pair + 256), wg[:])
+            name, cc, th, wg = piece
+            quantize(ops[name, "w", cc], slice(128 * th, 128 * th + 128), wg[:])
+
+        def weights(cc, th):
+            pieces = [weight_copy("w", cc, th, W_ENGINE[cc]), weight_copy("u", cc, th, "s")]
+            for piece in pieces:
+                weight_quantize(piece)
 
         acc = {}
         live = {}
 
         def gates_matmul(i):
-            g, cc = divmod(i, C)
-            cols = slice(128 * cc, 128 * cc + 128)
+            cc, g = ORDER[i]
             xq, hq = ops["x", g], ops["h", g]
-            acc[0] = bank("acc0")
-            mx(acc[0][:], ops["w", RESET], cols, xq, True, False)
-            mx(acc[0][:], ops["u", RESET], cols, hq, False, True)
-            acc[1] = bank("acc1")
-            mx(acc[1][:], ops["u", CAND], cols, hq, True, True)
-            acc[2] = bank("acc2")
-            mx(acc[2][:], ops["w", CAND], cols, xq, True, True)
-            acc[3] = bank("acc3")
-            mx(acc[3][:], ops["w", UPDATE], cols, xq, True, False)
-            mx(acc[3][:], ops["u", UPDATE], cols, hq, False, True)
+            wq, uq = ops["w", "w", cc], ops["u", "w", cc]
+            reset, update, cand = slice(0, 128), slice(128, 256), slice(256, 384)
+            acc[i, 0] = bank("acc0")
+            mx(acc[i, 0][:], wq, reset, xq, True, False)
+            mx(acc[i, 0][:], uq, reset, hq, False, True)
+            acc[i, 1] = bank("acc1")
+            mx(acc[i, 1][:], uq, cand, hq, True, True)
+            acc[i, 2] = bank("acc2")
+            mx(acc[i, 2][:], wq, cand, xq, True, True)
+            acc[i, 3] = bank("acc3")
+            mx(acc[i, 3][:], wq, update, xq, True, False)
+            mx(acc[i, 3][:], uq, update, hq, False, True)
 
         def ew(name, bufs):
             return pool.tile([P, 512], F32, name=name, bufs=bufs)
@@ -209,33 +231,33 @@ def tile_gru_station_readout_f4_kernel(
 
         def gate_r(i):
             r = ew("r_gate", 2)
-            nc.scalar.activation(r[:], acc[0][:], ACT.Sigmoid, bias=vcol(i % C))
+            nc.scalar.activation(r[:], acc[i, 0][:], ACT.Sigmoid, bias=vcol(ORDER[i][0]))
             live["r", i] = r
 
         def gate_z(i):
             z = ew("z_gate", 3)
-            nc.scalar.activation(z[:], acc[3][:], ACT.Sigmoid, bias=vcol(4 + i % C))
+            nc.scalar.activation(z[:], acc[i, 3][:], ACT.Sigmoid, bias=vcol(4 + ORDER[i][0]))
             live["z", i] = z
 
         def step_s1(i):
             s1 = ew("s1", 2)
             nc.vector.scalar_tensor_tensor(
-                out=s1[:], in0=acc[1][:], scalar=vcol(12 + i % C), in1=live["r", i][:], op0=ALU.add, op1=ALU.mult
+                out=s1[:], in0=acc[i, 1][:], scalar=vcol(12 + ORDER[i][0]), in1=live["r", i][:], op0=ALU.add, op1=ALU.mult
             )
             live["s1", i] = s1
 
         def step_s2(i):
             s2 = ew("s2", 2)
-            nc.vector.tensor_tensor(out=s2[:], in0=acc[2][:], in1=live["s1", i][:], op=ALU.add)
+            nc.vector.tensor_tensor(out=s2[:], in0=acc[i, 2][:], in1=live["s1", i][:], op=ALU.add)
             live["s2", i] = s2
 
         def step_n(i):
             n = ew("n_cand", 4)
-            nc.scalar.activation(n[:], live["s2", i][:], ACT.Tanh, bias=vcol(8 + i % C))
+            nc.scalar.activation(n[:], live["s2", i][:], ACT.Tanh, bias=vcol(8 + ORDER[i][0]))
             live["n", i] = n
 
         def h_transposes(i):
-            g, cc = divmod(i, C)
+            cc, g = ORDER[i]
             ht = bank("ht", 1, BF16)
             for t in range(4):
                 nc.tensor.transpose(
@@ -248,7 +270,7 @@ def tile_gru_station_readout_f4_kernel(
         def step_d(i):
             d = ew("diff", 2)
             nc.vector.scalar_tensor_tensor(
-                out=d[:], in0=live["ht", i][:], scalar=vcol(16 + i % C), in1=live["n", i][:],
+                out=d[:], in0=live["ht", i][:], scalar=vcol(16 + ORDER[i][0]), in1=live["n", i][:],
                 op0=ALU.mult, op1=ALU.subtract,
             )
             live["d", i] = d
@@ -270,68 +292,126 @@ def tile_gru_station_readout_f4_kernel(
             live["hb", i] = hb
 
         h_out = h_new.rearrange("(g p t) d -> g p t d", p=P, t=4)
-        hn = {}
 
         def state_copy(i):
-            g, cc = divmod(i, C)
-            if cc == 0:
-                hn[g] = pool.tile([P, 4, 512], F32, name="hn", bufs=2)
-            nc.scalar.copy(
-                hn[g][:, :, 128 * cc : 128 * cc + 128], live["hb", i][:].rearrange("p (t j) -> p t j", t=4)
-            )
+            hn = pool.tile([P, 4, P], F32, name="hn", bufs=4)
+            nc.scalar.copy(hn[:], live["hb", i][:].rearrange("p (t j) -> p t j", t=4))
+            live["hn", i] = hn
 
-        def state_store(g):
-            nc.sync.dma_start(out=h_out[g], in_=hn[g][:])
+        def state_store(i):
+            cc, g = ORDER[i]
+            nc.sync.dma_start(out=h_out[g][:, :, 128 * cc : 128 * cc + 128], in_=live["hn", i][:])
 
-        def step_m(i, engine):
-            g, cc = divmod(i, C)
+        def step_m(i):
+            cc, g = ORDER[i]
             mg = pool.tile([P, 512], BF16, name="m_grouped", bufs=3, align_bytes=64)
-            if engine == "v":
-                source = live["hb", i][:].rearrange("p (t j) -> p j t", t=4)
-                nc.vector.tensor_tensor(
-                    out=mg[:].rearrange("p (j t) -> p j t", t=4), in0=source,
-                    in1=gain_f[:, g, :].unsqueeze(1).to_broadcast([P, P, 4]), op=ALU.mult,
-                )
-            else:
-                source = hn[g][:, :, 128 * cc : 128 * cc + 128].rearrange("p t j -> p j t")
-                nc.gpsimd.tensor_tensor(
-                    out=mg[:].rearrange("p (j t) -> p j t", t=4), in0=source,
-                    in1=gain_f[:, g, :].unsqueeze(1).to_broadcast([P, P, 4]), op=ALU.mult,
-                )
+            nc.vector.tensor_tensor(
+                out=mg[:].rearrange("p (j t) -> p j t", t=4),
+                in0=live["hb", i][:].rearrange("p (t j) -> p j t", t=4),
+                in1=gain_f[:, g, :].unsqueeze(1).to_broadcast([P, P, 4]),
+                op=ALU.mult,
+            )
             live["m", i] = mg
 
         def quantize_m(i):
-            g, cc = divmod(i, C)
-            if cc == 0:
-                ops["m", g] = operand(const, "m" + str(g), 1)
-            quantize(ops["m", g], slice(128 * cc, 128 * cc + 128), live["m", i][:])
+            cc, g = ORDER[i]
+            codes = const.tile([P, P], U32, name="m_codes" + str(i), align_bytes=64)
+            scales = const.tile([P, P], U8, name="m_scales" + str(i), align_bytes=64)
+            ops["m", cc, g] = (codes, scales)
+            quantize(ops["m", cc, g], slice(0, 128), live["m", i][:])
 
         y_out = y.rearrange("(p s) d -> p s d", s=S)
-        y_banks = ("acc0", "acc1", "acc2", "acc3", "tp", "tp", "ht", "hb")
-        y_acc = {}
 
-        def y_passes(s, groups):
-            if s not in y_acc:
-                y_acc[s] = bank(y_banks[s], 2 if y_banks[s] == "tp" else 1)
-            for g in groups:
-                mx(y_acc[s][:], ops["p", s], slice(128 * g, 128 * g + 128), ops["m", g], g == 0, g == G - 1)
+        def y_pass(out, s, cc, g):
+            mx(out, ops["p", s], slice(128 * g, 128 * g + 128), ops["m", cc, g], g == 0, g == G - 1)
 
-        def y_store(s):
-            ys = pool.tile([P, 512], F32, name="y_rows", bufs=8)
-            if s % 2:
-                nc.vector.tensor_scalar(
-                    out=ys[:], in0=y_acc[s][:], scalar1=o_col[:, s : s + 1], scalar2=None, op0=ALU.add
+        def y_unit_passes(quad, cc):
+            yb = bank("tp", 2)
+            for k in range(4):
+                for g in range(G):
+                    y_pass(yb[:, 128 * k : 128 * k + 128], 4 * quad + k, cc, g)
+            return quad, cc, yb
+
+        def y_unit_store(unit, engine):
+            quad, cc, yb = unit
+            ys = pool.tile([P, 4, P], F32, name="y_rows", bufs=3)
+            if engine == "v":
+                nc.vector.tensor_tensor(
+                    out=ys[:],
+                    in0=yb[:].rearrange("p (k n) -> p k n", k=4),
+                    in1=o_col[:, 4 * quad : 4 * quad + 4].unsqueeze(2).to_broadcast([P, 4, P]),
+                    op=ALU.add,
                 )
             else:
-                nc.scalar.activation(ys[:], y_acc[s][:], ACT.Identity, bias=o_col[:, s : s + 1])
-            nc.sync.dma_start(out=y_out[:, s, :], in_=ys[:])
+                for k in range(4):
+                    nc.scalar.activation(
+                        ys[:, k, :], yb[:, 128 * k : 128 * k + 128], ACT.Identity,
+                        bias=o_col[:, 4 * quad + k : 4 * quad + k + 1],
+                    )
+            nc.sync.dma_start(out=y_out[:, 4 * quad : 4 * quad + 4, 128 * cc : 128 * cc + 128], in_=ys[:])
 
-        units = {1: (("x", 1),), 2: (("h", 1),), 4: (("p", 0),), 5: (("x", 2),), 6: (("h", 2),), 7: (("p", 1),),
-                 8: (("p", 2),), 9: (("x", 3),), 10: (("h", 3),), 11: (("p", 3),), 12: (("p", 4),), 13: (("p", 5),),
-                 14: (("p", 6), ("p", 7))}
-        counts = [0, 0, 1, 1, 1, 1, 1, 1, 1, 1, 1, 1, 3, 3, 0, 0]
         products = [(k // 2, k % 2) for k in range(16)]
-        late_weights = {0: (RESET, CAND), 1: (UPDATE,)}
+        pending = []
+        y_open = []
+
+        def unit_work(key):
+            for half in range(2):
+                unit = unit_transposes(key, unit_rows(key), half)
+                unit_copy("v" if key in EARLY and half == 1 else "s", unit)
+            if key in EARLY:
+                quantize_grouped(key)
+
+        def do_step(name, i):
+            keys = UNITS.get(i, ())
+            if name == "r":
+                gate_r(i)
+            elif name == "s1":
+                step_s1(i)
+            elif name == "z":
+                gate_z(i)
+            elif name == "s2":
+                step_s2(i)
+            elif name == "m" and i > 1:
+                step_m(i - 2)
+            elif name == "u0":
+                for key in keys[:1]:
+                    unit_work(key)
+            elif name == "u1":
+                for key in keys[1:]:
+                    unit_work(key)
+            elif name == "ht" and i > 0:
+                h_transposes(i)
+            elif name == "nq" and i > 0:
+                state_transposes(i - 1)
+            elif name == "w":
+                for cc, th in WEIGHT_SLOTS.get(i, ()):
+                    weights(cc, th)
+            elif name == "n":
+                step_n(i)
+            elif name == "ys":
+                for unit in y_open:
+                    y_unit_store(unit, "s")
+                y_open.clear()
+            elif name == "hc" and i > 0:
+                state_copy(i - 1)
+                state_store(i - 1)
+            elif name == "mq" and i > 1:
+                quantize_m(i - 2)
+            elif name == "quant":
+                for old in pending:
+                    quantize_grouped(old)
+                pending.clear()
+                pending.extend(key for key in keys if key not in EARLY)
+            elif name == "prod":
+                for k in range(COUNTS[i]):
+                    product(*products.pop(0))
+            elif name == "d":
+                step_d(i)
+                step_q(i, nc.gpsimd if i < TILES - 1 else nc.vector)
+            elif name == "mx" and i + 1 < TILES:
+                gates_matmul(i + 1)
+            elif name == "yp":
+                y_open.extend(y_unit_passes(quad, cc) for quad, cc in Y_SLOTS.get(i, ()))
 
         with tc.manual_schedule(
             engines={mybir.EngineType.PE, mybir.EngineType.Activation, mybir.EngineType.DVE, mybir.EngineType.Pool}
@@ -343,75 +423,51 @@ def tile_gru_station_readout_f4_kernel(
             quantize_grouped(("x", 0))
             quantize_grouped(("h", 0))
             nc.gpsimd.tensor_copy(out=gain_f[:], in_=gain_b[:])
+            vec_ps = bank("ht", 1, BF16)
+            nc.tensor.transpose(vec_ps[:, 0:128], vec_rows[:], ident_b[:])
+            nc.scalar.copy(vec[:], vec_ps[:, 0:128])
             for th in (RESET, CAND, UPDATE):
-                wp = weight_copy("w", th, 0, "v")
-                up = weight_copy("u", th, 0, "s")
-                weight_quantize(wp)
-                weight_quantize(up)
-                if th == RESET:
-                    vec_ps = bank("ht", 1, BF16)
-                    nc.tensor.transpose(vec_ps[:, 0:128], vec_rows[:], ident_b[:])
-                    nc.scalar.copy(vec[:], vec_ps[:, 0:128])
+                weights(0, th)
             gates_matmul(0)
             h_transposes(0)
 
             last = TILES - 1
-            pending = []
             for i in range(TILES):
-                keys = units.get(i, ())
-                gate_r(i)
-                step_s1(i)
-                gate_z(i)
-                if i > 1:
-                    step_m(i - 2, M_ENGINE[i - 2])
-                step_s2(i)
-                for key in keys:
-                    for half in range(2):
-                        unit = unit_transposes(key, unit_rows(key), half)
-                        unit_copy("s", unit)
-                if i > 0:
-                    h_transposes(i)
-                    state_transposes(i - 1)
-                step_n(i)
-                if i > 0:
-                    state_copy(i - 1)
-                if i > 1:
-                    quantize_m(i - 2)
-                    if i % C == 1 and i > C:
-                        state_store(i // C - 1)
-                for old in pending:
-                    quantize_grouped(old)
-                pending = []
-                for th in late_weights.get(i, ()):
-                    wp = weight_copy("w", th, 1, "v")
-                    up = weight_copy("u", th, 1, "s")
-                    weight_quantize(wp)
-                    weight_quantize(up)
-                for k in range(counts[i]):
-                    s, half = products.pop(0)
-                    product(s, half)
-                step_d(i)
-                step_q(i, nc.gpsimd if i < last else nc.vector)
-                pending.extend(keys)
-                if i + 1 < TILES:
-                    gates_matmul(i + 1)
-                else:
-                    for s in (4, 5, 0, 1):
-                        y_passes(s, range(G - 1))
-
-            step_m(last - 1, "v")
+                for name in SLOT:
+                    do_step(name, i)
+            step_m(last - 1)
             quantize_m(last - 1)
             for old in pending:
                 quantize_grouped(old)
+            for unit in y_open:
+                y_unit_store(unit, "s")
+            for quad, cc in Y_SLOTS.get(TILES, ()):
+                y_unit_store(y_unit_passes(quad, cc), "s")
+            y_banks = ("acc0", "acc1", "acc2", "acc3", "ht")
+            y_tail = []
             state_transposes(last)
-            step_m(last, "v")
+            step_m(last)
             quantize_m(last)
+            for s in range(5):
+                y_tail.append(bank(y_banks[s])[:, 0:128])
             state_copy(last)
-            state_store(G - 1)
-            for s in (2, 3, 6):
-                y_passes(s, range(G - 1))
-            for s in range(7):
-                y_passes(s, (G - 1,))
-                y_store(s)
-            y_passes(7, range(G))
-            y_store(7)
+            state_store(last)
+            y_tail.append(bank("tp", 2)[:, 0:128])
+            y_tail.append(bank("tp", 2)[:, 0:128])
+            y_tail.append(bank("hb")[:, 0:128])
+            for s in range(S - 1):
+                for g in range(G - 1):
+                    y_pass(y_tail[s], s, C - 1, g)
+            for quad in range(2):
+                ys = pool.tile([P, 4, P], F32, name="y_rows", bufs=3)
+                for k in range(4):
+                    s = 4 * quad + k
+                    for g in range(G - 1 if s < S - 1 else 0, G):
+                        y_pass(y_tail[s], s, C - 1, g)
+                    if k % 2:
+                        nc.vector.tensor_scalar(
+                            out=ys[:, k, :], in0=y_tail[s], scalar1=o_col[:, s : s + 1], scalar2=None, op0=ALU.add
+                        )
+                    else:
+                        nc.scalar.activation(ys[:, k, :], y_tail[s], ACT.Identity, bias=o_col[:, s : s + 1])
+                nc.sync.dma_start(out=y_out[:, 4 * quad : 4 * quad + 4, 128 * (C - 1) : D], in_=ys[:])

@@ -22,14 +22,15 @@ S = 8
 TILES = G * C
 RESET, UPDATE, CAND = 0, 1, 2
 WBUFS = 4
-XBUFS = 4
+XBUFS = 2
+PBUFS = 3
 ORDER = [(cc, g) for g in range(G) for cc in range(2)] + [(cc, g) for cc in range(2, C) for g in range(G)]
-EARLY = (('h', 1),)
-UNITS = {1: (('h', 1), ('h', 2)), 2: (('x', 2), ('x', 3)), 9: (('p', 4),), 3: (('h', 3),), 12: (('p', 6),), 8: (('p', 3),), 4: (('p', 0),), 5: (('p', 1),), 13: (('p', 7),), 10: (('p', 5),), 7: (('p', 2),), 0: (('x', 1),)}
-COUNTS = [0, 2, 1, 1, 1, 2, 1, 2, 1, 1, 1, 1, 2, 0, 0, 0]
-WEIGHT_SLOTS = {0: ((1, 0), (1, 2), (1, 1)), 6: ((3, 2), (2, 1)), 8: ((3, 0),), 7: ((3, 1),), 3: ((2, 2),), 5: ((2, 0),)}
-Y_SLOTS = {13: ((0, 2),), 14: ((1, 0),), 16: ((0, 1), (1, 2), (1, 1)), 10: ((0, 0),)}
-SLOT = 'r s1 m z u1 s2 quant w ys u0 ht n prod d mq nq mx yp hc'.split()
+EARLY = (('h', 1), ('h', 2), ('x', 2))
+UNITS = {2: (('h', 2),), 9: (('p', 4),), 3: (('h', 3),), 12: (('p', 6),), 4: (('p', 0),), 0: (('x', 1), ('h', 1), ('x', 2)), 14: (('p', 7),), 1: (('x', 3),), 6: (('p', 2),), 5: (('p', 1),), 8: (('p', 3),), 10: (('p', 5),)}
+COUNTS = [0, 3, 0, 1, 2, 1, 2, 0, 2, 1, 1, 1, 1, 1, 0, 0]
+WEIGHT_SLOTS = {0: ((1, 2), (1, 0), (1, 1)), 6: ((2, 0),), 7: ((3, 0), (3, 2)), 5: ((2, 1),), 4: ((2, 2),), 11: ((3, 1),)}
+Y_SLOTS = {12: ((1, 1),), 14: ((2, 1), (0, 2)), 10: ((0, 1),), 16: ((1, 2), (3, 1))}
+SLOT = 'r s1 m s2 quant w u0 u1 ys prod mx0 ht z mq n mx1 nq yp mx2 hc d mx3'.split()
 W_ENGINE = "vvss"
 
 
@@ -89,16 +90,17 @@ def tile_gru_station_readout_f4_kernel(
             nc.sync.dma_start(out=raw[:], in_=src.rearrange("(g p t) k -> g p t k", p=P, t=4)[g])
             raws[name, g] = raw
 
-        def load_weight(name, src, cc):
-            raw = pool.tile([P, 12, 128], BF16, name=name + "_raw", bufs=WBUFS)
+        def load_weight(name, src, first, count):
+            raw = const.tile([P, 12, 128 * count], BF16, name=name + "_raw" + str(first))
             nc.sync.dma_start(
                 out=raw[:],
-                in_=src.rearrange("(p j) (th n) -> p (j th) n", j=4, th=3)[:, :, 128 * cc : 128 * cc + 128],
+                in_=src.rearrange("(p j) (th n) -> p (j th) n", j=4, th=3)[:, :, 128 * first : 128 * (first + count)],
             )
-            raws[name, "w", cc] = raw
+            for k in range(count):
+                raws[name, "w", first + k] = raw[:, :, 128 * k : 128 * k + 128]
 
         def load_p(pair):
-            raw = pool.tile([P, 2, N], U8, name="p_raw", bufs=4)
+            raw = pool.tile([P, 2, N], U8, name="p_raw", bufs=PBUFS)
             nc.sync.dma_start(
                 out=raw[:], in_=p_bytes.rearrange("(p s) k -> p s k", s=S)[:, 2 * pair : 2 * pair + 2, :]
             )
@@ -116,10 +118,10 @@ def tile_gru_station_readout_f4_kernel(
         nc.scalar.dma_start(out=vec_rows[16:20, :], in_=carry.rearrange("(r m) -> r m", m=P))
         nc.gpsimd.dma_start(out=gain_b[:], in_=gain.rearrange("(g p t) -> p g t", p=P, t=4))
         nc.gpsimd.dma_start(out=o_col[:], in_=o.rearrange("(p s) -> p s", s=S))
-        load_weight("w", w, 0)
-        load_weight("u", u, 0)
-        load_weight("w", w, 1)
-        load_weight("u", u, 1)
+        load_weight("w", w, 0, 1)
+        load_weight("u", u, 0, 1)
+        load_weight("w", w, 1, 1)
+        load_weight("u", u, 1, 1)
         load_rows("x", x, 1, XBUFS)
         load_rows("h", h, 1, 4)
         load_rows("x", x, 2, XBUFS)
@@ -132,11 +134,9 @@ def tile_gru_station_readout_f4_kernel(
         load_rows("h", h, 3, 4)
         load_p(1)
         load_p(2)
-        load_weight("w", w, 2)
-        load_weight("u", u, 2)
+        load_weight("w", w, 2, 2)
+        load_weight("u", u, 2, 2)
         load_p(3)
-        load_weight("w", w, 3)
-        load_weight("u", u, 3)
 
         ops = {}
         grouped = {}
@@ -171,10 +171,10 @@ def tile_gru_station_readout_f4_kernel(
             ops[key] = operand(const, key[0] + str(key[1]), 1)
             quantize(ops[key], slice(0, 512), grouped[key][:])
 
-        def product(s, half):
+        def product(s, half, count):
             if half == 0:
                 raws["p_rows", s] = pool.tile([P, N], BF16, name="p_rows", bufs=2, align_bytes=64)
-            cols = slice(1024 * half, 1024 * half + 1024)
+            cols = slice(1024 * half, 1024 * (half + count))
             nc.vector.tensor_tensor(
                 out=raws["p_rows", s][:, cols],
                 in0=raws["p", s // 2][:, s % 2, cols].bitcast(FP8),
@@ -182,46 +182,38 @@ def tile_gru_station_readout_f4_kernel(
                 op=ALU.mult,
             )
 
-        def weight_copy(name, cc, th, engine):
-            if (name, "w", cc) not in ops:
-                codes = pool.tile([P, 384], U32, name=name + "_w_codes", bufs=3, align_bytes=64)
-                scales = pool.tile([P, 384], U8, name=name + "_w_scales", bufs=3, align_bytes=64)
-                ops[name, "w", cc] = (codes, scales)
-            wg = pool.tile([P, 512], BF16, name="weight_grouped", bufs=6, align_bytes=64)
-            copy(
-                engine,
-                wg[:].rearrange("p (m j) -> p m j", j=4),
-                raws[name, "w", cc][:].rearrange("p (j th) m -> p th m j", th=3)[:, th],
-            )
-            return name, cc, th, wg
-
-        def weight_quantize(piece):
-            name, cc, th, wg = piece
-            quantize(ops[name, "w", cc], slice(128 * th, 128 * th + 128), wg[:])
-
         def weights(cc, th):
-            pieces = [weight_copy("w", cc, th, W_ENGINE[cc]), weight_copy("u", cc, th, "s")]
-            for piece in pieces:
-                weight_quantize(piece)
+            wg = pool.tile([P, 1024], BF16, name="weight_grouped", bufs=3, align_bytes=64)
+            for k, name in enumerate(("w", "u")):
+                copy(
+                    W_ENGINE[cc] if name == "w" else "s",
+                    wg[:, 512 * k : 512 * k + 512].rearrange("p (m j) -> p m j", j=4),
+                    raws[name, "w", cc].rearrange("p (j th) m -> p th m j", th=3)[:, th],
+                )
+            codes = pool.tile([P, 256], U32, name="weight_codes" + str(th), bufs=3, align_bytes=64)
+            scales = pool.tile([P, 256], U8, name="weight_scales" + str(th), bufs=3, align_bytes=64)
+            ops["wu", cc, th] = (codes, scales)
+            quantize(ops["wu", cc, th], slice(0, 256), wg[:])
 
         acc = {}
         live = {}
 
-        def gates_matmul(i):
+        def gates_matmul(i, part):
             cc, g = ORDER[i]
             xq, hq = ops["x", g], ops["h", g]
-            wq, uq = ops["w", "w", cc], ops["u", "w", cc]
-            reset, update, cand = slice(0, 128), slice(128, 256), slice(256, 384)
-            acc[i, 0] = bank("acc0")
-            mx(acc[i, 0][:], wq, reset, xq, True, False)
-            mx(acc[i, 0][:], uq, reset, hq, False, True)
-            acc[i, 1] = bank("acc1")
-            mx(acc[i, 1][:], uq, cand, hq, True, True)
-            acc[i, 2] = bank("acc2")
-            mx(acc[i, 2][:], wq, cand, xq, True, True)
-            acc[i, 3] = bank("acc3")
-            mx(acc[i, 3][:], wq, update, xq, True, False)
-            mx(acc[i, 3][:], uq, update, hq, False, True)
+            wcols, ucols = slice(0, 128), slice(128, 256)
+            acc[i, part] = bank("acc" + str(part))
+            out = acc[i, part][:]
+            if part == 0:
+                mx(out, ops["wu", cc, RESET], wcols, xq, True, False)
+                mx(out, ops["wu", cc, RESET], ucols, hq, False, True)
+            elif part == 1:
+                mx(out, ops["wu", cc, CAND], ucols, hq, True, True)
+            elif part == 2:
+                mx(out, ops["wu", cc, CAND], wcols, xq, True, True)
+            else:
+                mx(out, ops["wu", cc, UPDATE], wcols, xq, True, False)
+                mx(out, ops["wu", cc, UPDATE], ucols, hq, False, True)
 
         def ew(name, bufs):
             return pool.tile([P, 512], F32, name=name, bufs=bufs)
@@ -260,10 +252,12 @@ def tile_gru_station_readout_f4_kernel(
             cc, g = ORDER[i]
             ht = bank("ht", 1, BF16)
             for t in range(4):
-                nc.tensor.transpose(
+                nc.tensor.matmul(
                     ht[:, 128 * t : 128 * t + 128],
-                    raws["h", g][:, t, 128 * cc : 128 * cc + 128],
-                    ident_b[:],
+                    lhsT=raws["h", g][:, t, 128 * cc : 128 * cc + 128],
+                    rhs=ident_b[:],
+                    start=True,
+                    stop=True,
                 )
             live["ht", i] = ht
 
@@ -293,62 +287,86 @@ def tile_gru_station_readout_f4_kernel(
 
         h_out = h_new.rearrange("(g p t) d -> g p t d", p=P, t=4)
 
+        def partner(i):
+            return ORDER[i][0] if ORDER[i][0] < 2 else None
+
         def state_copy(i):
-            hn = pool.tile([P, 4, P], F32, name="hn", bufs=4)
-            nc.scalar.copy(hn[:], live["hb", i][:].rearrange("p (t j) -> p t j", t=4))
-            live["hn", i] = hn
+            k = partner(i)
+            if k is None:
+                hn = pool.tile([P, 4, P], F32, name="hn", bufs=3)
+                live["hn", i] = hn
+                out = hn[:]
+            else:
+                if k == 0:
+                    live["hn", i] = pool.tile([P, 4, 2 * P], F32, name="hn_pair", bufs=2)
+                else:
+                    live["hn", i] = live["hn", i - 1]
+                out = live["hn", i][:, :, 128 * k : 128 * k + 128]
+            nc.scalar.copy(out, live["hb", i][:].rearrange("p (t j) -> p t j", t=4))
 
         def state_store(i):
             cc, g = ORDER[i]
-            nc.sync.dma_start(out=h_out[g][:, :, 128 * cc : 128 * cc + 128], in_=live["hn", i][:])
+            if partner(i) is None:
+                nc.sync.dma_start(out=h_out[g][:, :, 128 * cc : 128 * cc + 128], in_=live["hn", i][:])
+            elif cc == 1:
+                nc.sync.dma_start(out=h_out[g][:, :, 0:256], in_=live["hn", i][:])
 
         def step_m(i):
             cc, g = ORDER[i]
-            mg = pool.tile([P, 512], BF16, name="m_grouped", bufs=3, align_bytes=64)
+            k = partner(i)
+            if k is None:
+                live["m", i] = pool.tile([P, 512], BF16, name="m_grouped", bufs=3, align_bytes=64)
+            elif k == 0:
+                live["m", i] = pool.tile([P, 1024], BF16, name="m_pair", bufs=2, align_bytes=64)
+            else:
+                live["m", i] = live["m", i - 1]
+            mg = live["m", i][:, 512 * (k or 0) : 512 * (k or 0) + 512]
             nc.vector.tensor_tensor(
-                out=mg[:].rearrange("p (j t) -> p j t", t=4),
+                out=mg.rearrange("p (j t) -> p j t", t=4),
                 in0=live["hb", i][:].rearrange("p (t j) -> p j t", t=4),
                 in1=gain_f[:, g, :].unsqueeze(1).to_broadcast([P, P, 4]),
                 op=ALU.mult,
             )
-            live["m", i] = mg
 
         def quantize_m(i):
             cc, g = ORDER[i]
-            codes = const.tile([P, P], U32, name="m_codes" + str(i), align_bytes=64)
-            scales = const.tile([P, P], U8, name="m_scales" + str(i), align_bytes=64)
+            k = partner(i)
+            if k == 0:
+                return
+            width = 128 if k is None else 256
+            codes = const.tile([P, width], U32, name="m_codes" + str(i), align_bytes=64)
+            scales = const.tile([P, width], U8, name="m_scales" + str(i), align_bytes=64)
             ops["m", cc, g] = (codes, scales)
-            quantize(ops["m", cc, g], slice(0, 128), live["m", i][:])
+            quantize(ops["m", cc, g], slice(0, width), live["m", i][:])
 
         y_out = y.rearrange("(p s) d -> p s d", s=S)
 
         def y_pass(out, s, cc, g):
             mx(out, ops["p", s], slice(128 * g, 128 * g + 128), ops["m", cc, g], g == 0, g == G - 1)
 
-        def y_unit_passes(quad, cc):
+        def y_unit_passes(part, cc):
+            width = 256 if cc == 1 else 128
+            count = 512 // width
             yb = bank("tp", 2)
-            for k in range(4):
+            for k in range(count):
                 for g in range(G):
-                    y_pass(yb[:, 128 * k : 128 * k + 128], 4 * quad + k, cc, g)
-            return quad, cc, yb
+                    y_pass(yb[:, width * k : width * k + width], count * part + k, cc, g)
+            return part, cc, yb
 
         def y_unit_store(unit, engine):
-            quad, cc, yb = unit
-            ys = pool.tile([P, 4, P], F32, name="y_rows", bufs=3)
-            if engine == "v":
-                nc.vector.tensor_tensor(
-                    out=ys[:],
-                    in0=yb[:].rearrange("p (k n) -> p k n", k=4),
-                    in1=o_col[:, 4 * quad : 4 * quad + 4].unsqueeze(2).to_broadcast([P, 4, P]),
-                    op=ALU.add,
-                )
-            else:
-                for k in range(4):
-                    nc.scalar.activation(
-                        ys[:, k, :], yb[:, 128 * k : 128 * k + 128], ACT.Identity,
-                        bias=o_col[:, 4 * quad + k : 4 * quad + k + 1],
-                    )
-            nc.sync.dma_start(out=y_out[:, 4 * quad : 4 * quad + 4, 128 * cc : 128 * cc + 128], in_=ys[:])
+            part, cc, yb = unit
+            width = 256 if cc == 1 else 128
+            count = 512 // width
+            ys = pool.tile([P, 512], F32, name="y_rows", bufs=3)
+            for k in range(count):
+                s = count * part + k
+                cols = slice(width * k, width * k + width)
+                nc.scalar.activation(ys[:, cols], yb[:, cols], ACT.Identity, bias=o_col[:, s : s + 1])
+            first = 128 * (cc + 1) - width
+            nc.sync.dma_start(
+                out=y_out[:, count * part : count * part + count, first : first + width],
+                in_=ys[:].rearrange("p (k n) -> p k n", k=count),
+            )
 
         products = [(k // 2, k % 2) for k in range(16)]
         pending = []
@@ -403,13 +421,19 @@ def tile_gru_station_readout_f4_kernel(
                 pending.clear()
                 pending.extend(key for key in keys if key not in EARLY)
             elif name == "prod":
-                for k in range(COUNTS[i]):
-                    product(*products.pop(0))
+                left = COUNTS[i]
+                while left:
+                    s, half = products[0]
+                    count = 2 if half == 0 and left > 1 else 1
+                    product(s, half, count)
+                    for k in range(count):
+                        products.pop(0)
+                    left -= count
             elif name == "d":
                 step_d(i)
                 step_q(i, nc.gpsimd if i < TILES - 1 else nc.vector)
-            elif name == "mx" and i + 1 < TILES:
-                gates_matmul(i + 1)
+            elif name in ("mx0", "mx1", "mx2", "mx3") and i + 1 < TILES:
+                gates_matmul(i + 1, int(name[2]))
             elif name == "yp":
                 y_open.extend(y_unit_passes(quad, cc) for quad, cc in Y_SLOTS.get(i, ()))
 
@@ -428,7 +452,8 @@ def tile_gru_station_readout_f4_kernel(
             nc.scalar.copy(vec[:], vec_ps[:, 0:128])
             for th in (RESET, CAND, UPDATE):
                 weights(0, th)
-            gates_matmul(0)
+            for part in (0, 1, 2, 3):
+                gates_matmul(0, part)
             h_transposes(0)
 
             last = TILES - 1
@@ -459,15 +484,18 @@ def tile_gru_station_readout_f4_kernel(
                 for g in range(G - 1):
                     y_pass(y_tail[s], s, C - 1, g)
             for quad in range(2):
-                ys = pool.tile([P, 4, P], F32, name="y_rows", bufs=3)
+                ys = pool.tile([P, 512], F32, name="y_rows", bufs=3)
                 for k in range(4):
                     s = 4 * quad + k
                     for g in range(G - 1 if s < S - 1 else 0, G):
                         y_pass(y_tail[s], s, C - 1, g)
                     if k % 2:
                         nc.vector.tensor_scalar(
-                            out=ys[:, k, :], in0=y_tail[s], scalar1=o_col[:, s : s + 1], scalar2=None, op0=ALU.add
+                            out=ys[:, 128 * k : 128 * k + 128], in0=y_tail[s], scalar1=o_col[:, s : s + 1], scalar2=None, op0=ALU.add
                         )
                     else:
-                        nc.scalar.activation(ys[:, k, :], y_tail[s], ACT.Identity, bias=o_col[:, s : s + 1])
-                nc.sync.dma_start(out=y_out[:, 4 * quad : 4 * quad + 4, 128 * (C - 1) : D], in_=ys[:])
+                        nc.scalar.activation(ys[:, 128 * k : 128 * k + 128], y_tail[s], ACT.Identity, bias=o_col[:, s : s + 1])
+                nc.sync.dma_start(
+                    out=y_out[:, 4 * quad : 4 * quad + 4, 128 * (C - 1) : D],
+                    in_=ys[:].rearrange("p (k n) -> p k n", k=4),
+                )

from contextlib import ExitStack

import concourse.mybir as mybir
from concourse.masks import make_identity

N, I, D, R = 2048, 512, 512, 1024
FLOPS = 2 * N * (I + D) * 3 * D + 2 * R * N * D

F32 = mybir.dt.float32
BF16 = mybir.dt.bfloat16
U32 = mybir.dt.uint32
U8 = mybir.dt.uint8
FP8 = mybir.dt.float8_e4m3fn
FP8X4 = mybir.dt.float8_e4m3fn_x4
ACT = mybir.ActivationFunctionType
ALU = mybir.AluOpType

P = 128
G = 4
C = 4
S = 8
TILES = G * C
RESET, UPDATE, CAND = 0, 1, 2
WBUFS = 4
XBUFS = 2
PBUFS = 3
ORDER = [(cc, g) for g in range(G) for cc in range(2)] + [(cc, g) for cc in range(2, C) for g in range(G)]
EARLY = (('h', 1), ('h', 2), ('x', 2))
UNITS = {2: (('h', 2),), 9: (('p', 4),), 3: (('h', 3),), 12: (('p', 6),), 4: (('p', 0),), 0: (('x', 1), ('h', 1), ('x', 2)), 14: (('p', 7),), 1: (('x', 3),), 6: (('p', 2),), 5: (('p', 1),), 8: (('p', 3),), 10: (('p', 5),)}
COUNTS = [0, 3, 0, 1, 2, 1, 2, 0, 2, 1, 1, 1, 1, 1, 0, 0]
WEIGHT_SLOTS = {0: ((1, 2), (1, 0), (1, 1)), 6: ((2, 0),), 7: ((3, 0), (3, 2)), 5: ((2, 1),), 4: ((2, 2),), 11: ((3, 1),)}
Y_SLOTS = {12: ((1, 1),), 14: ((2, 1), (0, 2)), 10: ((0, 1),), 16: ((1, 2), (3, 1))}
SLOT = 'r s1 m s2 quant w u0 u1 ys prod mx0 ht z mq n mx1 nq yp mx2 hc d mx3'.split()
W_ENGINE = "vvss"


def tile_gru_station_readout_f4_kernel(
    tc, x, h, w, u, b, c, carry, gain, p_bytes, p_scale, o, y, h_new
):
    nc = tc.nc
    with ExitStack() as ctx:
        const = ctx.enter_context(tc.tile_pool(name="const", bufs=1))
        pool = ctx.enter_context(tc.tile_pool(name="pool", bufs=2))
        psum = ctx.enter_context(tc.psum_pool(name="psum", bufs=1))

        ident = const.tile([P, P], F32, name="ident")
        ident_b = const.tile([P, P], BF16, name="ident_b")
        vec_rows = const.tile([P, P], BF16, name="vec_rows")
        vec = const.tile([P, P], F32, name="vec")
        gain_b = const.tile([P, G, 4], BF16, name="gain_b")
        gain_f = const.tile([P, G, 4], F32, name="gain_f")
        o_col = const.tile([P, S], BF16, name="o_col")
        scale_rows = const.tile([P, N], F32, name="scale_rows")
        warm = const.tile([P, 1], F32, name="warm")

        def bank(tag, bufs=1, dtype=F32):
            return psum.tile([P, 512], dtype, name="bank_" + tag, tag=tag, bufs=bufs)

        def copy(engine, out, in_):
            if engine == "s":
                nc.scalar.copy(out, in_)
            else:
                nc.vector.tensor_copy(out=out, in_=in_)

        def mx(out, lhs, lhs_cols, rhs, start, stop):
            nc.tensor.matmul_mx(
                out=out,
                lhsT=lhs[0][:, lhs_cols].bitcast(FP8X4),
                lhsT_scale=lhs[1][:, lhs_cols],
                rhs=rhs[0][:].bitcast(FP8X4),
                rhs_scale=rhs[1][:],
                start=start,
                stop=stop,
            )

        def operand(home, tag, bufs):
            codes = home.tile([P, 512], U32, name=tag + "_codes", bufs=bufs, align_bytes=64)
            scales = home.tile([P, 512], U8, name=tag + "_scales", bufs=bufs, align_bytes=64)
            return codes, scales

        def quantize(target, cols, in_):
            nc.vector.quantize_mx(
                out=target[0][:, cols].bitcast(FP8X4), scales=target[1][:, cols], in_=in_
            )

        raws = {}

        def load_rows(name, src, g, bufs):
            raw = pool.tile([P, 4, 512], BF16, name=name + "_raw", bufs=bufs)
            nc.sync.dma_start(out=raw[:], in_=src.rearrange("(g p t) k -> g p t k", p=P, t=4)[g])
            raws[name, g] = raw

        def load_weight(name, src, first, count):
            raw = const.tile([P, 12, 128 * count], BF16, name=name + "_raw" + str(first))
            nc.sync.dma_start(
                out=raw[:],
                in_=src.rearrange("(p j) (th n) -> p (j th) n", j=4, th=3)[:, :, 128 * first : 128 * (first + count)],
            )
            for k in range(count):
                raws[name, "w", first + k] = raw[:, :, 128 * k : 128 * k + 128]

        def load_p(pair):
            raw = pool.tile([P, 2, N], U8, name="p_raw", bufs=PBUFS)
            nc.sync.dma_start(
                out=raw[:], in_=p_bytes.rearrange("(p s) k -> p s k", s=S)[:, 2 * pair : 2 * pair + 2, :]
            )
            raws["p", pair] = raw

        nc.vector.memset(warm[:], 0.0)
        nc.vector.memset(vec_rows[:], 0.0)
        nc.scalar.activation(warm[:], warm[:], ACT.Sigmoid)
        make_identity(nc, ident[:])
        nc.vector.tensor_copy(out=ident_b[:], in_=ident[:])
        load_rows("x", x, 0, XBUFS)
        load_rows("h", h, 0, 4)
        nc.scalar.dma_start(out=vec_rows[0:12, :], in_=b.rearrange("(r m) -> r m", m=P))
        nc.scalar.dma_start(out=vec_rows[12:16, :], in_=c.rearrange("(r m) -> r m", m=P))
        nc.scalar.dma_start(out=vec_rows[16:20, :], in_=carry.rearrange("(r m) -> r m", m=P))
        nc.gpsimd.dma_start(out=gain_b[:], in_=gain.rearrange("(g p t) -> p g t", p=P, t=4))
        nc.gpsimd.dma_start(out=o_col[:], in_=o.rearrange("(p s) -> p s", s=S))
        load_weight("w", w, 0, 1)
        load_weight("u", u, 0, 1)
        load_weight("w", w, 1, 1)
        load_weight("u", u, 1, 1)
        load_rows("x", x, 1, XBUFS)
        load_rows("h", h, 1, 4)
        load_rows("x", x, 2, XBUFS)
        load_rows("h", h, 2, 4)
        nc.sync.dma_start(
            out=scale_rows[:], in_=p_scale.rearrange("o k -> (o k)").partition_broadcast(P)
        )
        load_p(0)
        load_rows("x", x, 3, XBUFS)
        load_rows("h", h, 3, 4)
        load_p(1)
        load_p(2)
        load_weight("w", w, 2, 2)
        load_weight("u", u, 2, 2)
        load_p(3)

        ops = {}
        grouped = {}

        def unit_transposes(key, rows, half):
            if half == 0:
                grouped[key] = pool.tile([P, 2048], BF16, name=key[0] + "_grouped", bufs=2, align_bytes=64)
            words = rows.bitcast(F32)
            tp = bank("tp", 2)
            for k in range(4):
                base = 256 * (2 * half + k // 2) + k % 2
                end = 256 * (2 * half + k // 2) + 256
                nc.tensor.transpose(tp[:, 128 * k : 128 * k + 128], words[:, base:end:2], ident[:])
            return key, half, tp

        def unit_copy(engine, unit):
            key, half, tp = unit
            copy(
                engine,
                grouped[key][:].bitcast(F32)[:, 512 * half : 512 * half + 512].rearrange(
                    "p (a r e) -> p a r e", a=2, e=2
                ),
                tp[:].rearrange("p (a e r) -> p a r e", a=2, e=2),
            )

        def unit_rows(key):
            if key[0] == "p":
                return raws["p_rows", key[1]][:]
            return raws[key][:].rearrange("p t k -> p (t k)")

        def quantize_grouped(key):
            ops[key] = operand(const, key[0] + str(key[1]), 1)
            quantize(ops[key], slice(0, 512), grouped[key][:])

        def product(s, half, count):
            if half == 0:
                raws["p_rows", s] = pool.tile([P, N], BF16, name="p_rows", bufs=2, align_bytes=64)
            cols = slice(1024 * half, 1024 * (half + count))
            nc.vector.tensor_tensor(
                out=raws["p_rows", s][:, cols],
                in0=raws["p", s // 2][:, s % 2, cols].bitcast(FP8),
                in1=scale_rows[:, cols],
                op=ALU.mult,
            )

        def weights(cc, th):
            wg = pool.tile([P, 1024], BF16, name="weight_grouped", bufs=3, align_bytes=64)
            for k, name in enumerate(("w", "u")):
                copy(
                    W_ENGINE[cc] if name == "w" else "s",
                    wg[:, 512 * k : 512 * k + 512].rearrange("p (m j) -> p m j", j=4),
                    raws[name, "w", cc].rearrange("p (j th) m -> p th m j", th=3)[:, th],
                )
            codes = pool.tile([P, 256], U32, name="weight_codes" + str(th), bufs=3, align_bytes=64)
            scales = pool.tile([P, 256], U8, name="weight_scales" + str(th), bufs=3, align_bytes=64)
            ops["wu", cc, th] = (codes, scales)
            quantize(ops["wu", cc, th], slice(0, 256), wg[:])

        acc = {}
        live = {}

        def gates_matmul(i, part):
            cc, g = ORDER[i]
            xq, hq = ops["x", g], ops["h", g]
            wcols, ucols = slice(0, 128), slice(128, 256)
            acc[i, part] = bank("acc" + str(part))
            out = acc[i, part][:]
            if part == 0:
                mx(out, ops["wu", cc, RESET], wcols, xq, True, False)
                mx(out, ops["wu", cc, RESET], ucols, hq, False, True)
            elif part == 1:
                mx(out, ops["wu", cc, CAND], ucols, hq, True, True)
            elif part == 2:
                mx(out, ops["wu", cc, CAND], wcols, xq, True, True)
            else:
                mx(out, ops["wu", cc, UPDATE], wcols, xq, True, False)
                mx(out, ops["wu", cc, UPDATE], ucols, hq, False, True)

        def ew(name, bufs):
            return pool.tile([P, 512], F32, name=name, bufs=bufs)

        def vcol(r):
            return vec[:, r : r + 1]

        def gate_r(i):
            r = ew("r_gate", 2)
            nc.scalar.activation(r[:], acc[i, 0][:], ACT.Sigmoid, bias=vcol(ORDER[i][0]))
            live["r", i] = r

        def gate_z(i):
            z = ew("z_gate", 3)
            nc.scalar.activation(z[:], acc[i, 3][:], ACT.Sigmoid, bias=vcol(4 + ORDER[i][0]))
            live["z", i] = z

        def step_s1(i):
            s1 = ew("s1", 2)
            nc.vector.scalar_tensor_tensor(
                out=s1[:], in0=acc[i, 1][:], scalar=vcol(12 + ORDER[i][0]), in1=live["r", i][:], op0=ALU.add, op1=ALU.mult
            )
            live["s1", i] = s1

        def step_s2(i):
            s2 = ew("s2", 2)
            nc.vector.tensor_tensor(out=s2[:], in0=acc[i, 2][:], in1=live["s1", i][:], op=ALU.add)
            live["s2", i] = s2

        def step_n(i):
            n = ew("n_cand", 4)
            nc.scalar.activation(n[:], live["s2", i][:], ACT.Tanh, bias=vcol(8 + ORDER[i][0]))
            live["n", i] = n

        def h_transposes(i):
            cc, g = ORDER[i]
            ht = bank("ht", 1, BF16)
            for t in range(4):
                nc.tensor.matmul(
                    ht[:, 128 * t : 128 * t + 128],
                    lhsT=raws["h", g][:, t, 128 * cc : 128 * cc + 128],
                    rhs=ident_b[:],
                    start=True,
                    stop=True,
                )
            live["ht", i] = ht

        def step_d(i):
            d = ew("diff", 2)
            nc.vector.scalar_tensor_tensor(
                out=d[:], in0=live["ht", i][:], scalar=vcol(16 + ORDER[i][0]), in1=live["n", i][:],
                op0=ALU.mult, op1=ALU.subtract,
            )
            live["d", i] = d

        def step_q(i, engine):
            q = ew("zdiff", 3)
            engine.tensor_tensor(out=q[:], in0=live["z", i][:], in1=live["d", i][:], op=ALU.mult)
            live["q", i] = q

        def state_transposes(i):
            hb = bank("hb")
            for t in range(4):
                cols = slice(128 * t, 128 * t + 128)
                for k, part in enumerate(("n", "q")):
                    nc.tensor.matmul(
                        hb[:, cols], lhsT=live[part, i][:, cols], rhs=ident[:],
                        start=(k == 0), stop=(k == 1), is_transpose=True,
                    )
            live["hb", i] = hb

        h_out = h_new.rearrange("(g p t) d -> g p t d", p=P, t=4)

        def partner(i):
            return ORDER[i][0] if ORDER[i][0] < 2 else None

        def state_copy(i):
            k = partner(i)
            if k is None:
                hn = pool.tile([P, 4, P], F32, name="hn", bufs=3)
                live["hn", i] = hn
                out = hn[:]
            else:
                if k == 0:
                    live["hn", i] = pool.tile([P, 4, 2 * P], F32, name="hn_pair", bufs=2)
                else:
                    live["hn", i] = live["hn", i - 1]
                out = live["hn", i][:, :, 128 * k : 128 * k + 128]
            nc.scalar.copy(out, live["hb", i][:].rearrange("p (t j) -> p t j", t=4))

        def state_store(i):
            cc, g = ORDER[i]
            if partner(i) is None:
                nc.sync.dma_start(out=h_out[g][:, :, 128 * cc : 128 * cc + 128], in_=live["hn", i][:])
            elif cc == 1:
                nc.sync.dma_start(out=h_out[g][:, :, 0:256], in_=live["hn", i][:])

        def step_m(i):
            cc, g = ORDER[i]
            k = partner(i)
            if k is None:
                live["m", i] = pool.tile([P, 512], BF16, name="m_grouped", bufs=3, align_bytes=64)
            elif k == 0:
                live["m", i] = pool.tile([P, 1024], BF16, name="m_pair", bufs=2, align_bytes=64)
            else:
                live["m", i] = live["m", i - 1]
            mg = live["m", i][:, 512 * (k or 0) : 512 * (k or 0) + 512]
            nc.vector.tensor_tensor(
                out=mg.rearrange("p (j t) -> p j t", t=4),
                in0=live["hb", i][:].rearrange("p (t j) -> p j t", t=4),
                in1=gain_f[:, g, :].unsqueeze(1).to_broadcast([P, P, 4]),
                op=ALU.mult,
            )

        def quantize_m(i):
            cc, g = ORDER[i]
            k = partner(i)
            if k == 0:
                return
            width = 128 if k is None else 256
            codes = const.tile([P, width], U32, name="m_codes" + str(i), align_bytes=64)
            scales = const.tile([P, width], U8, name="m_scales" + str(i), align_bytes=64)
            ops["m", cc, g] = (codes, scales)
            quantize(ops["m", cc, g], slice(0, width), live["m", i][:])

        y_out = y.rearrange("(p s) d -> p s d", s=S)

        def y_pass(out, s, cc, g):
            mx(out, ops["p", s], slice(128 * g, 128 * g + 128), ops["m", cc, g], g == 0, g == G - 1)

        def y_unit_passes(part, cc):
            width = 256 if cc == 1 else 128
            count = 512 // width
            yb = bank("tp", 2)
            for k in range(count):
                for g in range(G):
                    y_pass(yb[:, width * k : width * k + width], count * part + k, cc, g)
            return part, cc, yb

        def y_unit_store(unit, engine):
            part, cc, yb = unit
            width = 256 if cc == 1 else 128
            count = 512 // width
            ys = pool.tile([P, 512], F32, name="y_rows", bufs=3)
            for k in range(count):
                s = count * part + k
                cols = slice(width * k, width * k + width)
                nc.scalar.activation(ys[:, cols], yb[:, cols], ACT.Identity, bias=o_col[:, s : s + 1])
            first = 128 * (cc + 1) - width
            nc.sync.dma_start(
                out=y_out[:, count * part : count * part + count, first : first + width],
                in_=ys[:].rearrange("p (k n) -> p k n", k=count),
            )

        products = [(k // 2, k % 2) for k in range(16)]
        pending = []
        y_open = []

        def unit_work(key):
            for half in range(2):
                unit = unit_transposes(key, unit_rows(key), half)
                unit_copy("v" if key in EARLY and half == 1 else "s", unit)
            if key in EARLY:
                quantize_grouped(key)

        def do_step(name, i):
            keys = UNITS.get(i, ())
            if name == "r":
                gate_r(i)
            elif name == "s1":
                step_s1(i)
            elif name == "z":
                gate_z(i)
            elif name == "s2":
                step_s2(i)
            elif name == "m" and i > 1:
                step_m(i - 2)
            elif name == "u0":
                for key in keys[:1]:
                    unit_work(key)
            elif name == "u1":
                for key in keys[1:]:
                    unit_work(key)
            elif name == "ht" and i > 0:
                h_transposes(i)
            elif name == "nq" and i > 0:
                state_transposes(i - 1)
            elif name == "w":
                for cc, th in WEIGHT_SLOTS.get(i, ()):
                    weights(cc, th)
            elif name == "n":
                step_n(i)
            elif name == "ys":
                for unit in y_open:
                    y_unit_store(unit, "s")
                y_open.clear()
            elif name == "hc" and i > 0:
                state_copy(i - 1)
                state_store(i - 1)
            elif name == "mq" and i > 1:
                quantize_m(i - 2)
            elif name == "quant":
                for old in pending:
                    quantize_grouped(old)
                pending.clear()
                pending.extend(key for key in keys if key not in EARLY)
            elif name == "prod":
                left = COUNTS[i]
                while left:
                    s, half = products[0]
                    count = 2 if half == 0 and left > 1 else 1
                    product(s, half, count)
                    for k in range(count):
                        products.pop(0)
                    left -= count
            elif name == "d":
                step_d(i)
                step_q(i, nc.gpsimd if i < TILES - 1 else nc.vector)
            elif name in ("mx0", "mx1", "mx2", "mx3") and i + 1 < TILES:
                gates_matmul(i + 1, int(name[2]))
            elif name == "yp":
                y_open.extend(y_unit_passes(quad, cc) for quad, cc in Y_SLOTS.get(i, ()))

        with tc.manual_schedule(
            engines={mybir.EngineType.PE, mybir.EngineType.Activation, mybir.EngineType.DVE, mybir.EngineType.Pool}
        ):
            for key in (("x", 0), ("h", 0)):
                for half in range(2):
                    unit = unit_transposes(key, unit_rows(key), half)
                    unit_copy("vs"[half], unit)
            quantize_grouped(("x", 0))
            quantize_grouped(("h", 0))
            nc.gpsimd.tensor_copy(out=gain_f[:], in_=gain_b[:])
            vec_ps = bank("ht", 1, BF16)
            nc.tensor.transpose(vec_ps[:, 0:128], vec_rows[:], ident_b[:])
            nc.scalar.copy(vec[:], vec_ps[:, 0:128])
            for th in (RESET, CAND, UPDATE):
                weights(0, th)
            for part in (0, 1, 2, 3):
                gates_matmul(0, part)
            h_transposes(0)

            last = TILES - 1
            for i in range(TILES):
                for name in SLOT:
                    do_step(name, i)
            step_m(last - 1)
            quantize_m(last - 1)
            for old in pending:
                quantize_grouped(old)
            for unit in y_open:
                y_unit_store(unit, "s")
            for quad, cc in Y_SLOTS.get(TILES, ()):
                y_unit_store(y_unit_passes(quad, cc), "s")
            y_banks = ("acc0", "acc1", "acc2", "acc3", "ht")
            y_tail = []
            state_transposes(last)
            step_m(last)
            quantize_m(last)
            for s in range(5):
                y_tail.append(bank(y_banks[s])[:, 0:128])
            state_copy(last)
            state_store(last)
            y_tail.append(bank("tp", 2)[:, 0:128])
            y_tail.append(bank("tp", 2)[:, 0:128])
            y_tail.append(bank("hb")[:, 0:128])
            for s in range(S - 1):
                for g in range(G - 1):
                    y_pass(y_tail[s], s, C - 1, g)
            for quad in range(2):
                ys = pool.tile([P, 512], F32, name="y_rows", bufs=3)
                for k in range(4):
                    s = 4 * quad + k
                    for g in range(G - 1 if s < S - 1 else 0, G):
                        y_pass(y_tail[s], s, C - 1, g)
                    if k % 2:
                        nc.vector.tensor_scalar(
                            out=ys[:, 128 * k : 128 * k + 128], in0=y_tail[s], scalar1=o_col[:, s : s + 1], scalar2=None, op0=ALU.add
                        )
                    else:
                        nc.scalar.activation(ys[:, 128 * k : 128 * k + 128], y_tail[s], ACT.Identity, bias=o_col[:, s : s + 1])
                nc.sync.dma_start(
                    out=y_out[:, 4 * quad : 4 * quad + 4, 128 * (C - 1) : D],
                    in_=ys[:].rearrange("p (k n) -> p k n", k=4),
                )
